import numpy as np
import ml_dtypes


def mxq(x, axis, fmt="e4m3"):
    dtype, down = {"e4m3": (ml_dtypes.float8_e4m3fn, 7), "e5m2": (ml_dtypes.float8_e5m2, 14)}[fmt]
    v = np.moveaxis(np.asarray(x, np.float32).astype(ml_dtypes.bfloat16).astype(np.float64), axis, -1)
    blocks = v.reshape(v.shape[:-1] + (-1, 32))
    amax = np.abs(blocks).max(-1, keepdims=True)
    byte = np.maximum(np.where(amax > 0, np.frexp(amax)[1] - 1 + 127, 0) - down, 1)
    scale = np.exp2(byte - 127.0)
    codes = (blocks / scale).astype(np.float32).astype(dtype).astype(np.float64)
    return np.moveaxis((codes * scale).reshape(v.shape), -1, axis)


WIDE = False


def mx_kscale(k):
    if not WIDE:
        return np.ones(k)
    levels = np.array([10, -10, 5, -5, 0])
    if k % 512:
        return np.exp2(np.random.permutation(np.resize(levels, k // 32))).repeat(32)
    a = np.empty((k // 512, 16))
    for p in range(k // 512):
        a[p, :8] = np.random.permutation(np.resize(levels, 8))
        for g in range(8):
            far = levels[np.abs(levels - a[p, g]) >= 10]
            a[p, g + 8] = far[np.random.randint(len(far))]
    return np.exp2(a.ravel()).repeat(32)


def f64(x):
    return np.asarray(x).astype(np.float64)


def striped(idx):
    return np.tile(idx.reshape(-1, 16).T, (8, 1)).astype(np.uint16)


def unstriped(offs):
    return offs[:16].T.reshape(-1).astype(np.int64)


def striped8(idx):
    return np.concatenate([x.reshape(-1, 16).T for x in idx]).astype(np.uint16)


def runs(offs, k):
    lists = np.stack([offs[16 * r : 16 * r + 16].T.reshape(-1) for r in range(8)]).astype(np.int64)
    return lists[np.arange(k) % 512 // 64]


def pack_weight(w):
    k, n = w.shape
    w = f64(np.asarray(w, np.float32).astype(ml_dtypes.bfloat16)).reshape(k // 32, 32, n)
    amax = np.abs(w).max(1)
    byte = np.clip(np.where(amax > 0, np.frexp(amax)[1] - 1 + 127 - 7, 1), 1, 254)
    scaled = (w * np.exp2(127.0 - byte)[:, None, :]).reshape(k, n).astype(np.float32)
    words = np.ascontiguousarray(scaled.reshape(k // 512, 128, 4, n).transpose(0, 1, 3, 2)).astype(ml_dtypes.float8_e4m3fn).view(np.uint8)
    return words, np.ascontiguousarray(byte.astype(np.uint8).reshape(k // 512, 16, n))


def unpack_weight(words, scales):
    g, p, n, _ = words.shape
    vals = np.ascontiguousarray(words).view(ml_dtypes.float8_e4m3fn).astype(np.float64) * np.repeat(np.exp2(scales.astype(np.float64) - 127.0), 8, axis=1)[..., None]
    return vals.transpose(0, 1, 3, 2).reshape(g * 512, n)

def planes(y):
    n, m = y.shape
    v = y.astype(np.float32).astype(ml_dtypes.bfloat16).astype(np.float64).reshape(n // 32, 32, m)
    top = np.abs(v).max(1)
    byte = np.clip(np.where(top > 0, np.frexp(top)[1] - 1 + 127 - 7, 1), 1, 254)
    codes = (v * np.exp2(127.0 - byte)[:, None, :]).reshape(n, m).astype(np.float32).astype(ml_dtypes.float8_e4m3fn).view(np.uint8)
    words = codes.reshape(n // 512, 128, 4, m).transpose(0, 1, 3, 2)
    return np.ascontiguousarray(words), np.ascontiguousarray(byte.astype(np.uint8).reshape(n // 512, 16, m))


K, T, S, N, G, H, U = 512, 2048, 512, 512, 2048, 512, 1024


def setup_inputs():
    n = np.random.standard_normal
    s = mx_kscale(K)[:, None]
    u = mx_kscale(S)
    packed_xT = pack_weight(n((K, T)) * s)
    packed_dT = pack_weight(n((K, G)) / s)
    packed_w1 = pack_weight(n((H, N)) / np.sqrt(H) / u[:, None])
    return {
        "x_words": packed_xT[0],
        "x_scales": packed_xT[1],
        "d_words": packed_dT[0],
        "d_scales": packed_dT[1],
        "gn": (np.random.uniform(0.5, 1.5, (H, 1)) * u[:, None]).astype(np.float32),
        "w1_words": packed_w1[0],
        "w1_scales": packed_w1[1],
        "mem": n((N, U)).astype(np.float32),
        "offs": striped(np.random.permutation(T)[:S]),
        "kidx": striped8(np.random.randint(0, G, (8, H))),
        "n1": striped8(np.stack([np.random.permutation(S) for _ in range(8)])),
        "n2": striped8(np.stack([np.random.permutation(S) for _ in range(8)])),
        "n3": striped8(np.stack([np.random.permutation(U)[:S] for _ in range(8)])),
    }


def reference(x_words, x_scales, d_words, d_scales, gn, w1_words, w1_scales, mem, offs, kidx, n1, n2, n3):
    d_kidx = unpack_weight(d_words, d_scales)[np.arange(K)[:, None], runs(kidx, K)]
    xq = unpack_weight(x_words, x_scales)[:, unstriped(offs)]
    s = 0.0625 * (d_kidx.T @ xq)
    z = f64(gn) * ((np.tanh(s[np.arange(H)[:, None], runs(n1, H)] - s)) * (s[np.arange(H)[:, None], runs(n2, H)]))
    h = unpack_weight(w1_words, w1_scales).T @ mxq(z, 0, "e4m3")
    nw = np.maximum(h, 0.5 * (f64(mem)[np.arange(N)[:, None], runs(n3, N)]))
    out = f64(mem).copy()
    out[np.arange(N)[:, None], runs(n3, N)] = nw
    return (out,) + planes(out)

@@ -1,0 +1,209 @@
+from contextlib import ExitStack
+
+import concourse.mybir as mybir
+
+F32 = mybir.dt.float32
+BF16 = mybir.dt.bfloat16
+I32 = mybir.dt.int32
+U32 = mybir.dt.uint32
+U16 = mybir.dt.uint16
+U8 = mybir.dt.uint8
+FP8X4 = mybir.dt.float8_e4m3fn_x4
+ALU = mybir.AluOpType
+ACT = mybir.ActivationFunctionType
+
+P = 128
+PACK = 4
+TABLE = 2048
+S = 512
+U = 1024
+HALF = U // 2
+FLOPS = 2 * 2 * 512 * 512 * 512
+
+
+def tile_picked_keyfdifpagex_none_po_kernel(
+    tc, x_words, x_scales, d_words, d_scales, gn, w1_words, w1_scales, mem, offs, kidx, n1, n2, n3, out_0, out_1, out_2
+):
+    nc = tc.nc
+    with ExitStack() as ctx:
+        lists = ctx.enter_context(tc.tile_pool(name="lists", bufs=1))
+        pool = ctx.enter_context(tc.tile_pool(name="pool", bufs=1))
+        psum = ctx.enter_context(tc.psum_pool(name="psum", bufs=1))
+
+        def sb(shape, dtype, name, tag=None):
+            return pool.tile(shape, dtype, name=name, tag=tag or name, align_bytes=64)
+
+        def words_of(dram):
+            return dram[0].rearrange("p n t -> p (n t)").bitcast(I32)
+
+        d_sc_win = sb([P, TABLE], U8, "d_sc_win", "slot_a")
+        x_sc_win = sb([P, TABLE], U8, "x_sc_win", "slot_b")
+        nc.gpsimd.memset(d_sc_win[:].bitcast(I32), 0)
+        nc.vector.memset(x_sc_win[:].bitcast(I32), 0)
+        nc.scalar.dma_start(d_sc_win[:].bitcast(I32)[0:P:8, :], d_scales[0].bitcast(I32))
+        nc.scalar.dma_start(x_sc_win[:].bitcast(I32)[0:P:8, :], x_scales[0].bitcast(I32))
+
+        kidx_t = lists.tile([P, S // 16], U16, name="kidx_t")
+        offs_t = lists.tile([P, S // 16], U16, name="offs_t")
+        n1_t = lists.tile([P, S // 16], U16, name="n1_t")
+        n2_t = lists.tile([P, S // 16], U16, name="n2_t")
+        n3_t = lists.tile([P, S // 16], U16, name="n3_t")
+        d_win = sb([P, TABLE], U32, "d_win", "slot_c")
+        x_win = sb([P, TABLE], U32, "x_win", "slot_d")
+        gn_t = sb([P, PACK], F32, "gn_t")
+        nc.sync.dma_start(kidx_t[:], kidx)
+        nc.sync.dma_start(offs_t[:], offs)
+        nc.sync.dma_start(d_win[:].bitcast(I32), words_of(d_words))
+        nc.sync.dma_start(n1_t[:], n1)
+        nc.sync.dma_start(n2_t[:], n2)
+        nc.sync.dma_start(n3_t[:], n3)
+        nc.sync.dma_start(x_win[:].bitcast(I32), words_of(x_words))
+        nc.gpsimd.dma_start(gn_t[:], gn.rearrange("(p t) o -> p (t o)", t=PACK))
+
+        planes = sb([P, 2 * S], U8, "planes")
+        nc.vector.memset(planes[:].bitcast(I32), 0)
+        s_win = [sb([P, 2 * S], F32, f"s_win{t}") for t in range(PACK)]
+        for t in range(PACK):
+            eng = nc.vector if t % 2 == 0 else nc.gpsimd
+            eng.memset(s_win[t][:, S:], 0.0)
+        nc.scalar.activation(s_win[0][:, S : S + 1], s_win[0][:, S + 8 : S + 9], ACT.Tanh)
+
+        picked_sc = sb([P, 2 * S], U8, "picked_sc", "slot_e")
+        nc.vector.tensor_copy(picked_sc[:, :S], d_sc_win[:].indirect(kidx_t[:]))
+        nc.vector.tensor_copy(picked_sc[:, S:], x_sc_win[:].indirect(offs_t[:]))
+        for q in range(4):
+            nc.scalar.dma_start(
+                planes[:].bitcast(I32)[32 * q : 32 * q + 4, :], picked_sc[:].bitcast(I32)[32 * q : 32 * q + 32 : 8, :]
+            )
+        d_picked = sb([P, S], U32, "d_picked", "slot_f")
+        nc.vector.tensor_copy(d_picked[:], d_win[:].indirect(kidx_t[:]))
+
+        def deal(dst, src, run):
+            nc.vector.tensor_copy(
+                dst.rearrange("p (t c i) -> p c t i", t=PACK, i=run), src.rearrange("p (c i t) -> p c t i", t=PACK, i=run)
+            )
+
+        d_dealt = sb([P, S], U32, "d_dealt")
+        deal(d_dealt[:], d_picked[:], 4)
+        x_picked = sb([P, S], U32, "x_picked")
+        nc.vector.tensor_copy(x_picked[:], x_win[:].indirect(offs_t[:]))
+        d_sc_dealt = sb([P, S], U8, "d_sc_dealt")
+        deal(d_sc_dealt[:], planes[:, :S], 16)
+
+        mem_rows = mem.rearrange("(p t) u -> t p u", t=PACK)
+        out_rows = out_0.rearrange("(p t) u -> t p u", t=PACK)
+        page = [sb([P, U], F32, f"page{t}", "slot_" + "abcd"[t]) for t in range(PACK)]
+        for t in range(PACK):
+            nc.sync.dma_start(page[t][:], mem_rows[t])
+        w_words = sb([P, S], U32, "w_words", "slot_f")
+        nc.sync.dma_start(w_words[:].bitcast(I32), words_of(w1_words))
+        w_sc = sb([P, S], U8, "w_sc", "slot_e")
+        nc.gpsimd.memset(w_sc[:].bitcast(I32), 0)
+        for q in range(4):
+            nc.sync.dma_start(w_sc[:].bitcast(I32)[32 * q : 32 * q + 4, :], w1_scales[0, 4 * q : 4 * q + 4, :].bitcast(I32))
+
+        s_ps = [psum.tile([P, S], F32, name=f"s_ps{t}") for t in range(PACK)]
+        for t in range(PACK):
+            cols = slice(P * t, P * (t + 1))
+            nc.tensor.matmul_mx(
+                out=s_ps[t][:],
+                lhsT=d_dealt[:, cols].bitcast(FP8X4),
+                lhsT_scale=d_sc_dealt[:, cols],
+                rhs=x_picked[:].bitcast(FP8X4),
+                rhs_scale=planes[:, S:],
+                start=True,
+                stop=True,
+            )
+
+        old = [None] * PACK
+
+        def fetch_old(t, tag):
+            old[t] = sb([P, S], F32, f"old{t}", tag)
+            nc.vector.tensor_copy(old[t][:], page[t][:].indirect(n3_t[:]))
+
+        fetch_old(0, None)
+        fetch_old(1, None)
+
+        g_win = [sb([P, 2 * S], F32, f"g_win{t}") for t in range(PACK)]
+        diff = [sb([P, S], F32, f"diff{t}") for t in range(PACK)]
+        th = [sb([P, S], F32, f"th{t}") for t in range(PACK)]
+        z = sb([P, PACK, S], F32, "z")
+        zb = sb([P, S, PACK], BF16, "zb")
+
+        def first(t):
+            nc.scalar.activation(s_win[t][:, :S], s_ps[t][:], ACT.Copy, scale=0.0625)
+            nc.scalar.activation(g_win[t][:, S:], s_ps[t][:], ACT.Copy, scale=0.0625)
+            nc.vector.tensor_tensor(diff[t][:], s_win[t][:].indirect(n1_t[:]), g_win[t][:, S:], ALU.subtract)
+
+        def second(t):
+            nc.scalar.activation(th[t][:], diff[t][:], ACT.Tanh)
+            nc.scalar.activation(g_win[t][:, :S], s_win[t][:, :S], ACT.Copy, scale=gn_t[:, t : t + 1])
+            nc.vector.tensor_tensor(z[:, t, :], g_win[t][:].indirect(n2_t[:]), th[t][:], ALU.mult)
+            if t % 2 == 1:
+                nc.scalar.copy(
+                    zb[:, :, t - 1 : t + 1].rearrange("p (c i) t -> p c t i", i=4),
+                    z[:, t - 1 : t + 1, :].rearrange("p t (c i) -> p c t i", i=4),
+                )
+
+        first(0)
+        for t in range(PACK):
+            if t + 1 < PACK:
+                first(t + 1)
+            second(t)
+
+        w_sc_dealt = sb([P, S], U8, "w_sc_dealt")
+        deal(w_sc_dealt[:], w_sc[:], 16)
+        w_dealt = sb([P, S], U32, "w_dealt", "th3")
+        deal(w_dealt[:], w_words[:], 4)
+        fetch_old(2, "g_win3")
+
+        z_words = sb([P, S], U32, "z_words")
+        z_sc = sb([P, S], U8, "z_sc")
+        nc.vector.quantize_mx(out=z_words[:].bitcast(FP8X4), scales=z_sc[:], in_=zb[:].rearrange("p j t -> p (j t)"))
+        fetch_old(3, "zb")
+
+        h_ps = [psum.tile([P, S], F32, name=f"h_ps{t}") for t in range(PACK)]
+        for t in range(PACK):
+            cols = slice(P * t, P * (t + 1))
+            nc.tensor.matmul_mx(
+                out=h_ps[t][:],
+                lhsT=w_dealt[:, cols].bitcast(FP8X4),
+                lhsT_scale=w_sc_dealt[:, cols],
+                rhs=z_words[:].bitcast(FP8X4),
+                rhs_scale=z_sc[:],
+                start=True,
+                stop=True,
+            )
+
+        new = [sb([P, S], F32, f"new{t}") for t in range(PACK)]
+        yb = [sb([P, HALF, PACK], BF16, f"yb{h}") for h in range(2)]
+
+        def larger(t):
+            nc.vector.scalar_tensor_tensor(new[t][:], old[t][:], 0.5, h_ps[t][:], ALU.mult, ALU.max)
+
+        larger(0)
+        for t in range(PACK):
+            if t + 1 < PACK:
+                larger(t + 1)
+            nc.vector.tensor_copy(page[t][:].indirect(n3_t[:]), new[t][:])
+            nc.sync.dma_start(out_rows[t], page[t][:])
+            for h in range(2):
+                src = page[t][:, HALF * h : HALF * (h + 1)]
+                if t == 2 and h == 0:
+                    nc.scalar.copy(yb[h][:, :, 2:4], src.unsqueeze(2).to_broadcast([P, HALF, 2]))
+                elif t == 3 and h == 0:
+                    nc.vector.tensor_copy(yb[h][:, :, t], src)
+                else:
+                    nc.scalar.copy(yb[h][:, :, t], src)
+
+        y_words = sb([P, U], U32, "y_words")
+        y_sc = sb([P, U], U8, "y_sc")
+        for h in range(2):
+            cols = slice(HALF * h, HALF * (h + 1))
+            nc.vector.quantize_mx(
+                out=y_words[:, cols].bitcast(FP8X4), scales=y_sc[:, cols], in_=yb[h][:].rearrange("p j t -> p (j t)")
+            )
+            nc.sync.dma_start(words_of(out_1)[:, cols], y_words[:, cols].bitcast(I32))
+        for q in range(4):
+            eng = nc.scalar if q % 2 == 0 else nc.sync
+            eng.dma_start(out_2[0, 4 * q : 4 * q + 4, :].bitcast(I32), y_sc[:].bitcast(I32)[32 * q : 32 * q + 4, :])

@@ -18,6 +18,7 @@ TABLE = 2048
 S = 512
 U = 1024
 HALF = U // 2
+SPLIT = 640
 FLOPS = 2 * 2 * 512 * 512 * 512
 
 
@@ -40,8 +41,8 @@ def tile_picked_keyfdifpagex_none_po_kernel(
         x_sc_win = sb([P, TABLE], U8, "x_sc_win", "slot_b")
         nc.gpsimd.memset(d_sc_win[:].bitcast(I32), 0)
         nc.vector.memset(x_sc_win[:].bitcast(I32), 0)
-        nc.scalar.dma_start(d_sc_win[:].bitcast(I32)[0:P:8, :], d_scales[0].bitcast(I32))
-        nc.scalar.dma_start(x_sc_win[:].bitcast(I32)[0:P:8, :], x_scales[0].bitcast(I32))
+        nc.sync.dma_start(d_sc_win[:].bitcast(I32)[0:P:8, :], d_scales[0].bitcast(I32))
+        nc.sync.dma_start(x_sc_win[:].bitcast(I32)[0:P:8, :], x_scales[0].bitcast(I32))
 
         kidx_t = lists.tile([P, S // 16], U16, name="kidx_t")
         offs_t = lists.tile([P, S // 16], U16, name="offs_t")
@@ -53,10 +54,10 @@ def tile_picked_keyfdifpagex_none_po_kernel(
         gn_t = sb([P, PACK], F32, "gn_t")
         nc.sync.dma_start(kidx_t[:], kidx)
         nc.sync.dma_start(offs_t[:], offs)
-        nc.sync.dma_start(d_win[:].bitcast(I32), words_of(d_words))
         nc.sync.dma_start(n1_t[:], n1)
         nc.sync.dma_start(n2_t[:], n2)
         nc.sync.dma_start(n3_t[:], n3)
+        nc.sync.dma_start(d_win[:].bitcast(I32), words_of(d_words))
         nc.sync.dma_start(x_win[:].bitcast(I32), words_of(x_words))
         nc.gpsimd.dma_start(gn_t[:], gn.rearrange("(p t) o -> p (t o)", t=PACK))
 
@@ -68,36 +69,38 @@ def tile_picked_keyfdifpagex_none_po_kernel(
             eng.memset(s_win[t][:, S:], 0.0)
         nc.scalar.activation(s_win[0][:, S : S + 1], s_win[0][:, S + 8 : S + 9], ACT.Tanh)
 
-        picked_sc = sb([P, 2 * S], U8, "picked_sc", "slot_e")
+        picked_sc = sb([P, 2 * S], U8, "picked_sc", "slot_h")
         nc.vector.tensor_copy(picked_sc[:, :S], d_sc_win[:].indirect(kidx_t[:]))
         nc.vector.tensor_copy(picked_sc[:, S:], x_sc_win[:].indirect(offs_t[:]))
-        for q in range(4):
-            nc.scalar.dma_start(
-                planes[:].bitcast(I32)[32 * q : 32 * q + 4, :], picked_sc[:].bitcast(I32)[32 * q : 32 * q + 32 : 8, :]
-            )
-        d_picked = sb([P, S], U32, "d_picked", "slot_f")
-        nc.vector.tensor_copy(d_picked[:], d_win[:].indirect(kidx_t[:]))
 
         def deal(dst, src, run):
             nc.vector.tensor_copy(
                 dst.rearrange("p (t c i) -> p c t i", t=PACK, i=run), src.rearrange("p (c i t) -> p c t i", t=PACK, i=run)
             )
 
+        staged_sc = sb([P, 2 * S], U8, "staged_sc", "slot_e")
+        deal(staged_sc[:, :S], picked_sc[:, :S], 16)
+        nc.vector.tensor_copy(staged_sc[:, S:].bitcast(I32), picked_sc[:, S:].bitcast(I32))
+        for q in range(4):
+            nc.scalar.dma_start(
+                planes[:].bitcast(I32)[32 * q : 32 * q + 4, :], staged_sc[:].bitcast(I32)[32 * q : 32 * q + 32 : 8, :]
+            )
+        d_picked = sb([P, S], U32, "d_picked", "slot_f")
+        nc.vector.tensor_copy(d_picked[:], d_win[:].indirect(kidx_t[:]))
         d_dealt = sb([P, S], U32, "d_dealt")
         deal(d_dealt[:], d_picked[:], 4)
-        x_picked = sb([P, S], U32, "x_picked")
+        x_picked = sb([P, S], U32, "x_picked", "slot_g")
         nc.vector.tensor_copy(x_picked[:], x_win[:].indirect(offs_t[:]))
-        d_sc_dealt = sb([P, S], U8, "d_sc_dealt")
-        deal(d_sc_dealt[:], planes[:, :S], 16)
 
         mem_rows = mem.rearrange("(p t) u -> t p u", t=PACK)
         out_rows = out_0.rearrange("(p t) u -> t p u", t=PACK)
-        page = [sb([P, U], F32, f"page{t}", "slot_" + "abcd"[t]) for t in range(PACK)]
+        page = [sb([P, U], F32, f"page{t}", "slot_" + "hceg"[t]) for t in range(PACK)]
         for t in range(PACK):
-            nc.sync.dma_start(page[t][:], mem_rows[t])
-        w_words = sb([P, S], U32, "w_words", "slot_f")
+            eng = nc.scalar if t == 0 else nc.sync
+            eng.dma_start(page[t][:], mem_rows[t])
+        w_words = sb([P, S], U32, "w_words", "d_dealt")
         nc.sync.dma_start(w_words[:].bitcast(I32), words_of(w1_words))
-        w_sc = sb([P, S], U8, "w_sc", "slot_e")
+        w_sc = sb([P, S], U8, "w_sc", "slot_f")
         nc.gpsimd.memset(w_sc[:].bitcast(I32), 0)
         for q in range(4):
             nc.sync.dma_start(w_sc[:].bitcast(I32)[32 * q : 32 * q + 4, :], w1_scales[0, 4 * q : 4 * q + 4, :].bitcast(I32))
@@ -108,7 +111,7 @@ def tile_picked_keyfdifpagex_none_po_kernel(
             nc.tensor.matmul_mx(
                 out=s_ps[t][:],
                 lhsT=d_dealt[:, cols].bitcast(FP8X4),
-                lhsT_scale=d_sc_dealt[:, cols],
+                lhsT_scale=planes[:, cols],
                 rhs=x_picked[:].bitcast(FP8X4),
                 rhs_scale=planes[:, S:],
                 start=True,
@@ -117,12 +120,13 @@ def tile_picked_keyfdifpagex_none_po_kernel(
 
         old = [None] * PACK
 
-        def fetch_old(t, tag):
-            old[t] = sb([P, S], F32, f"old{t}", tag)
-            nc.vector.tensor_copy(old[t][:], page[t][:].indirect(n3_t[:]))
+        def fetch_old(t, dst):
+            old[t] = dst
+            nc.vector.tensor_copy(dst, page[t][:].indirect(n3_t[:]))
 
-        fetch_old(0, None)
-        fetch_old(1, None)
+        old_early = sb([P, 2, S], F32, "old_early", "slot_d")
+        fetch_old(0, old_early[:, 0, :])
+        fetch_old(1, old_early[:, 1, :])
 
         g_win = [sb([P, 2 * S], F32, f"g_win{t}") for t in range(PACK)]
         diff = [sb([P, S], F32, f"diff{t}") for t in range(PACK)]
@@ -155,12 +159,12 @@ def tile_picked_keyfdifpagex_none_po_kernel(
         deal(w_sc_dealt[:], w_sc[:], 16)
         w_dealt = sb([P, S], U32, "w_dealt", "th3")
         deal(w_dealt[:], w_words[:], 4)
-        fetch_old(2, "g_win3")
+        fetch_old(2, sb([P, S], F32, "old2", "g_win3")[:])
 
         z_words = sb([P, S], U32, "z_words")
         z_sc = sb([P, S], U8, "z_sc")
         nc.vector.quantize_mx(out=z_words[:].bitcast(FP8X4), scales=z_sc[:], in_=zb[:].rearrange("p j t -> p (j t)"))
-        fetch_old(3, "zb")
+        fetch_old(3, sb([P, S], F32, "old3", "zb")[:])
 
         h_ps = [psum.tile([P, S], F32, name=f"h_ps{t}") for t in range(PACK)]
         for t in range(PACK):
@@ -179,7 +183,7 @@ def tile_picked_keyfdifpagex_none_po_kernel(
         yb = [sb([P, HALF, PACK], BF16, f"yb{h}") for h in range(2)]
 
         def larger(t):
-            nc.vector.scalar_tensor_tensor(new[t][:], old[t][:], 0.5, h_ps[t][:], ALU.mult, ALU.max)
+            nc.vector.scalar_tensor_tensor(new[t][:], old[t], 0.5, h_ps[t][:], ALU.mult, ALU.max)
 
         larger(0)
         for t in range(PACK):
@@ -187,14 +191,16 @@ def tile_picked_keyfdifpagex_none_po_kernel(
                 larger(t + 1)
             nc.vector.tensor_copy(page[t][:].indirect(n3_t[:]), new[t][:])
             nc.sync.dma_start(out_rows[t], page[t][:])
-            for h in range(2):
-                src = page[t][:, HALF * h : HALF * (h + 1)]
-                if t == 2 and h == 0:
-                    nc.scalar.copy(yb[h][:, :, 2:4], src.unsqueeze(2).to_broadcast([P, HALF, 2]))
-                elif t == 3 and h == 0:
-                    nc.vector.tensor_copy(yb[h][:, :, t], src)
+            for c0, c1 in ((0, HALF), (HALF, SPLIT), (SPLIT, U)):
+                h = c0 // HALF
+                src = page[t][:, c0:c1]
+                dst = yb[h][:, c0 - HALF * h : c1 - HALF * h, :]
+                if t == 2 and c0 < SPLIT:
+                    nc.scalar.copy(dst[:, :, 2:4], src.unsqueeze(2).to_broadcast([P, c1 - c0, 2]))
+                elif t == 3 and c0 < SPLIT:
+                    nc.vector.tensor_copy(dst[:, :, t], src)
                 else:
-                    nc.scalar.copy(yb[h][:, :, t], src)
+                    nc.scalar.copy(dst[:, :, t], src)
 
         y_words = sb([P, U], U32, "y_words")
         y_sc = sb([P, U], U8, "y_sc")

@@ -52,13 +52,15 @@ def tile_picked_keyfdifpagex_none_po_kernel(
         d_win = sb([P, TABLE], U32, "d_win", "slot_c")
         x_win = sb([P, TABLE], U32, "x_win", "slot_d")
         gn_t = sb([P, PACK], F32, "gn_t")
+        w_words = sb([P, S], U32, "w_words")
+        nc.sync.dma_start(w_words[:].bitcast(I32), words_of(w1_words))
         nc.sync.dma_start(kidx_t[:], kidx)
         nc.sync.dma_start(offs_t[:], offs)
         nc.sync.dma_start(n1_t[:], n1)
         nc.sync.dma_start(n2_t[:], n2)
-        nc.sync.dma_start(n3_t[:], n3)
         nc.sync.dma_start(d_win[:].bitcast(I32), words_of(d_words))
         nc.sync.dma_start(x_win[:].bitcast(I32), words_of(x_words))
+        nc.sync.dma_start(n3_t[:], n3)
         nc.gpsimd.dma_start(gn_t[:], gn.rearrange("(p t) o -> p (t o)", t=PACK))
 
         planes = sb([P, 2 * S], U8, "planes")
@@ -69,14 +71,17 @@ def tile_picked_keyfdifpagex_none_po_kernel(
             eng.memset(s_win[t][:, S:], 0.0)
         nc.scalar.activation(s_win[0][:, S : S + 1], s_win[0][:, S + 8 : S + 9], ACT.Tanh)
 
-        picked_sc = sb([P, 2 * S], U8, "picked_sc", "slot_h")
-        nc.vector.tensor_copy(picked_sc[:, :S], d_sc_win[:].indirect(kidx_t[:]))
-        nc.vector.tensor_copy(picked_sc[:, S:], x_sc_win[:].indirect(offs_t[:]))
-
         def deal(dst, src, run):
             nc.vector.tensor_copy(
                 dst.rearrange("p (t c i) -> p c t i", t=PACK, i=run), src.rearrange("p (c i t) -> p c t i", t=PACK, i=run)
             )
+
+        w_dealt = sb([P, S], U32, "w_dealt")
+        deal(w_dealt[:], w_words[:], 4)
+
+        picked_sc = sb([P, 2 * S], U8, "picked_sc", "slot_h")
+        nc.vector.tensor_copy(picked_sc[:, :S], d_sc_win[:].indirect(kidx_t[:]))
+        nc.vector.tensor_copy(picked_sc[:, S:], x_sc_win[:].indirect(offs_t[:]))
 
         staged_sc = sb([P, 2 * S], U8, "staged_sc", "slot_e")
         deal(staged_sc[:, :S], picked_sc[:, :S], 16)
@@ -94,12 +99,10 @@ def tile_picked_keyfdifpagex_none_po_kernel(
 
         mem_rows = mem.rearrange("(p t) u -> t p u", t=PACK)
         out_rows = out_0.rearrange("(p t) u -> t p u", t=PACK)
-        page = [sb([P, U], F32, f"page{t}", "slot_" + "hceg"[t]) for t in range(PACK)]
+        page = [sb([P, U], F32, f"page{t}", "slot_" + "bhce"[t]) for t in range(PACK)]
         for t in range(PACK):
-            eng = nc.scalar if t == 0 else nc.sync
+            eng = nc.scalar if t < 2 else nc.sync
             eng.dma_start(page[t][:], mem_rows[t])
-        w_words = sb([P, S], U32, "w_words", "d_dealt")
-        nc.sync.dma_start(w_words[:].bitcast(I32), words_of(w1_words))
         w_sc = sb([P, S], U8, "w_sc", "slot_f")
         nc.gpsimd.memset(w_sc[:].bitcast(I32), 0)
         for q in range(4):
@@ -140,25 +143,23 @@ def tile_picked_keyfdifpagex_none_po_kernel(
             nc.vector.tensor_tensor(diff[t][:], s_win[t][:].indirect(n1_t[:]), g_win[t][:, S:], ALU.subtract)
 
         def second(t):
-            nc.scalar.activation(th[t][:], diff[t][:], ACT.Tanh)
             nc.scalar.activation(g_win[t][:, :S], s_win[t][:, :S], ACT.Copy, scale=gn_t[:, t : t + 1])
+            nc.scalar.activation(th[t][:], diff[t][:], ACT.Tanh)
             nc.vector.tensor_tensor(z[:, t, :], g_win[t][:].indirect(n2_t[:]), th[t][:], ALU.mult)
-            if t % 2 == 1:
-                nc.scalar.copy(
-                    zb[:, :, t - 1 : t + 1].rearrange("p (c i) t -> p c t i", i=4),
-                    z[:, t - 1 : t + 1, :].rearrange("p t (c i) -> p c t i", i=4),
-                )
 
         first(0)
         for t in range(PACK):
             if t + 1 < PACK:
                 first(t + 1)
             second(t)
+        for t in (0, 2):
+            nc.scalar.copy(
+                zb[:, :, t : t + 2].rearrange("p (c i) t -> p c t i", i=4),
+                z[:, t : t + 2, :].rearrange("p t (c i) -> p c t i", i=4),
+            )
 
-        w_sc_dealt = sb([P, S], U8, "w_sc_dealt")
+        w_sc_dealt = sb([P, S], U8, "w_sc_dealt", "th3")
         deal(w_sc_dealt[:], w_sc[:], 16)
-        w_dealt = sb([P, S], U32, "w_dealt", "th3")
-        deal(w_dealt[:], w_words[:], 4)
         fetch_old(2, sb([P, S], F32, "old2", "g_win3")[:])
 
         z_words = sb([P, S], U32, "z_words")
@@ -191,7 +192,7 @@ def tile_picked_keyfdifpagex_none_po_kernel(
                 larger(t + 1)
             nc.vector.tensor_copy(page[t][:].indirect(n3_t[:]), new[t][:])
             nc.sync.dma_start(out_rows[t], page[t][:])
-            for c0, c1 in ((0, HALF), (HALF, SPLIT), (SPLIT, U)):
+            for c0, c1 in ((0, HALF), (HALF, U)) if t < 2 else ((0, HALF), (HALF, SPLIT), (SPLIT, U)):
                 h = c0 // HALF
                 src = page[t][:, c0:c1]
                 dst = yb[h][:, c0 - HALF * h : c1 - HALF * h, :]
@@ -204,10 +205,13 @@ def tile_picked_keyfdifpagex_none_po_kernel(
 
         y_words = sb([P, U], U32, "y_words")
         y_sc = sb([P, U], U8, "y_sc")
-        for h in range(2):
-            cols = slice(HALF * h, HALF * (h + 1))
+        for c0, c1 in ((0, HALF), (HALF, 768), (768, U)):
+            cols = slice(c0, c1)
+            h = c0 // HALF
             nc.vector.quantize_mx(
-                out=y_words[:, cols].bitcast(FP8X4), scales=y_sc[:, cols], in_=yb[h][:].rearrange("p j t -> p (j t)")
+                out=y_words[:, cols].bitcast(FP8X4),
+                scales=y_sc[:, cols],
+                in_=yb[h][:, c0 - HALF * h : c1 - HALF * h, :].rearrange("p j t -> p (j t)"),
             )
             nc.sync.dma_start(words_of(out_1)[:, cols], y_words[:, cols].bitcast(I32))
         for q in range(4):

from contextlib import ExitStack

import concourse.mybir as mybir

F32 = mybir.dt.float32
BF16 = mybir.dt.bfloat16
I32 = mybir.dt.int32
U32 = mybir.dt.uint32
U16 = mybir.dt.uint16
U8 = mybir.dt.uint8
FP8X4 = mybir.dt.float8_e4m3fn_x4
ALU = mybir.AluOpType
ACT = mybir.ActivationFunctionType

P = 128
PACK = 4
TABLE = 2048
S = 512
U = 1024
HALF = U // 2
SPLIT = 640
FLOPS = 2 * 2 * 512 * 512 * 512


def tile_picked_keyfdifpagex_none_po_kernel(
    tc, x_words, x_scales, d_words, d_scales, gn, w1_words, w1_scales, mem, offs, kidx, n1, n2, n3, out_0, out_1, out_2
):
    nc = tc.nc
    with ExitStack() as ctx:
        lists = ctx.enter_context(tc.tile_pool(name="lists", bufs=1))
        pool = ctx.enter_context(tc.tile_pool(name="pool", bufs=1))
        psum = ctx.enter_context(tc.psum_pool(name="psum", bufs=1))

        def sb(shape, dtype, name, tag=None):
            return pool.tile(shape, dtype, name=name, tag=tag or name, align_bytes=64)

        def words_of(dram):
            return dram[0].rearrange("p n t -> p (n t)").bitcast(I32)

        d_sc_win = sb([P, TABLE], U8, "d_sc_win", "slot_a")
        x_sc_win = sb([P, TABLE], U8, "x_sc_win", "slot_b")
        nc.gpsimd.memset(d_sc_win[:].bitcast(I32), 0)
        nc.vector.memset(x_sc_win[:].bitcast(I32), 0)
        nc.sync.dma_start(d_sc_win[:].bitcast(I32)[0:P:8, :], d_scales[0].bitcast(I32))
        nc.sync.dma_start(x_sc_win[:].bitcast(I32)[0:P:8, :], x_scales[0].bitcast(I32))

        kidx_t = lists.tile([P, S // 16], U16, name="kidx_t")
        offs_t = lists.tile([P, S // 16], U16, name="offs_t")
        n1_t = lists.tile([P, S // 16], U16, name="n1_t")
        n2_t = lists.tile([P, S // 16], U16, name="n2_t")
        n3_t = lists.tile([P, S // 16], U16, name="n3_t")
        d_win = sb([P, TABLE], U32, "d_win", "slot_c")
        x_win = sb([P, TABLE], U32, "x_win", "slot_d")
        gn_t = sb([P, PACK], F32, "gn_t")
        w_words = sb([P, S], U32, "w_words")
        nc.sync.dma_start(w_words[:].bitcast(I32), words_of(w1_words))
        nc.sync.dma_start(kidx_t[:], kidx)
        nc.sync.dma_start(offs_t[:], offs)
        nc.sync.dma_start(n1_t[:], n1)
        nc.sync.dma_start(n2_t[:], n2)
        nc.sync.dma_start(d_win[:].bitcast(I32), words_of(d_words))
        nc.sync.dma_start(x_win[:].bitcast(I32), words_of(x_words))
        nc.sync.dma_start(n3_t[:], n3)
        nc.gpsimd.dma_start(gn_t[:], gn.rearrange("(p t) o -> p (t o)", t=PACK))

        planes = sb([P, 2 * S], U8, "planes")
        nc.vector.memset(planes[:].bitcast(I32), 0)
        s_win = [sb([P, 2 * S], F32, f"s_win{t}") for t in range(PACK)]
        for t in range(PACK):
            eng = nc.vector if t % 2 == 0 else nc.gpsimd
            eng.memset(s_win[t][:, S:], 0.0)
        nc.scalar.activation(s_win[0][:, S : S + 1], s_win[0][:, S + 8 : S + 9], ACT.Tanh)

        def deal(dst, src, run):
            nc.vector.tensor_copy(
                dst.rearrange("p (t c i) -> p c t i", t=PACK, i=run), src.rearrange("p (c i t) -> p c t i", t=PACK, i=run)
            )

        w_dealt = sb([P, S], U32, "w_dealt")
        deal(w_dealt[:], w_words[:], 4)

        picked_sc = sb([P, 2 * S], U8, "picked_sc", "slot_h")
        nc.vector.tensor_copy(picked_sc[:, :S], d_sc_win[:].indirect(kidx_t[:]))
        nc.vector.tensor_copy(picked_sc[:, S:], x_sc_win[:].indirect(offs_t[:]))

        staged_sc = sb([P, 2 * S], U8, "staged_sc", "slot_e")
        deal(staged_sc[:, :S], picked_sc[:, :S], 16)
        nc.vector.tensor_copy(staged_sc[:, S:].bitcast(I32), picked_sc[:, S:].bitcast(I32))
        for q in range(4):
            nc.scalar.dma_start(
                planes[:].bitcast(I32)[32 * q : 32 * q + 4, :], staged_sc[:].bitcast(I32)[32 * q : 32 * q + 32 : 8, :]
            )
        d_picked = sb([P, S], U32, "d_picked", "slot_f")
        nc.vector.tensor_copy(d_picked[:], d_win[:].indirect(kidx_t[:]))
        d_dealt = sb([P, S], U32, "d_dealt")
        deal(d_dealt[:], d_picked[:], 4)
        x_picked = sb([P, S], U32, "x_picked", "slot_g")
        nc.vector.tensor_copy(x_picked[:], x_win[:].indirect(offs_t[:]))

        mem_rows = mem.rearrange("(p t) u -> t p u", t=PACK)
        out_rows = out_0.rearrange("(p t) u -> t p u", t=PACK)
        page = [sb([P, U], F32, f"page{t}", "slot_" + "bhce"[t]) for t in range(PACK)]
        for t in range(PACK):
            eng = nc.scalar if t < 2 else nc.sync
            eng.dma_start(page[t][:], mem_rows[t])
        w_sc = sb([P, S], U8, "w_sc", "slot_f")
        nc.gpsimd.memset(w_sc[:].bitcast(I32), 0)
        for q in range(4):
            nc.sync.dma_start(w_sc[:].bitcast(I32)[32 * q : 32 * q + 4, :], w1_scales[0, 4 * q : 4 * q + 4, :].bitcast(I32))

        s_ps = [psum.tile([P, S], F32, name=f"s_ps{t}") for t in range(PACK)]
        for t in range(PACK):
            cols = slice(P * t, P * (t + 1))
            nc.tensor.matmul_mx(
                out=s_ps[t][:],
                lhsT=d_dealt[:, cols].bitcast(FP8X4),
                lhsT_scale=planes[:, cols],
                rhs=x_picked[:].bitcast(FP8X4),
                rhs_scale=planes[:, S:],
                start=True,
                stop=True,
            )

        old = [None] * PACK

        def fetch_old(t, dst):
            old[t] = dst
            nc.vector.tensor_copy(dst, page[t][:].indirect(n3_t[:]))

        old_early = sb([P, 2, S], F32, "old_early", "slot_d")
        fetch_old(0, old_early[:, 0, :])
        fetch_old(1, old_early[:, 1, :])

        g_win = [sb([P, 2 * S], F32, f"g_win{t}") for t in range(PACK)]
        diff = [sb([P, S], F32, f"diff{t}") for t in range(PACK)]
        th = [sb([P, S], F32, f"th{t}") for t in range(PACK)]
        z = sb([P, PACK, S], F32, "z")
        zb = sb([P, S, PACK], BF16, "zb")

        def first(t):
            nc.scalar.activation(s_win[t][:, :S], s_ps[t][:], ACT.Copy, scale=0.0625)
            nc.scalar.activation(g_win[t][:, S:], s_ps[t][:], ACT.Copy, scale=0.0625)
            nc.vector.tensor_tensor(diff[t][:], s_win[t][:].indirect(n1_t[:]), g_win[t][:, S:], ALU.subtract)

        def second(t):
            nc.scalar.activation(g_win[t][:, :S], s_win[t][:, :S], ACT.Copy, scale=gn_t[:, t : t + 1])
            nc.scalar.activation(th[t][:], diff[t][:], ACT.Tanh)
            nc.vector.tensor_tensor(z[:, t, :], g_win[t][:].indirect(n2_t[:]), th[t][:], ALU.mult)

        first(0)
        for t in range(PACK):
            if t + 1 < PACK:
                first(t + 1)
            second(t)
        for t in (0, 2):
            nc.scalar.copy(
                zb[:, :, t : t + 2].rearrange("p (c i) t -> p c t i", i=4),
                z[:, t : t + 2, :].rearrange("p t (c i) -> p c t i", i=4),
            )

        w_sc_dealt = sb([P, S], U8, "w_sc_dealt", "th3")
        deal(w_sc_dealt[:], w_sc[:], 16)
        fetch_old(2, sb([P, S], F32, "old2", "g_win3")[:])

        z_words = sb([P, S], U32, "z_words")
        z_sc = sb([P, S], U8, "z_sc")
        nc.vector.quantize_mx(out=z_words[:].bitcast(FP8X4), scales=z_sc[:], in_=zb[:].rearrange("p j t -> p (j t)"))
        fetch_old(3, sb([P, S], F32, "old3", "zb")[:])

        h_ps = [psum.tile([P, S], F32, name=f"h_ps{t}") for t in range(PACK)]
        for t in range(PACK):
            cols = slice(P * t, P * (t + 1))
            nc.tensor.matmul_mx(
                out=h_ps[t][:],
                lhsT=w_dealt[:, cols].bitcast(FP8X4),
                lhsT_scale=w_sc_dealt[:, cols],
                rhs=z_words[:].bitcast(FP8X4),
                rhs_scale=z_sc[:],
                start=True,
                stop=True,
            )

        new = [sb([P, S], F32, f"new{t}") for t in range(PACK)]
        yb = [sb([P, HALF, PACK], BF16, f"yb{h}") for h in range(2)]

        def larger(t):
            nc.vector.scalar_tensor_tensor(new[t][:], old[t], 0.5, h_ps[t][:], ALU.mult, ALU.max)

        larger(0)
        for t in range(PACK):
            if t + 1 < PACK:
                larger(t + 1)
            nc.vector.tensor_copy(page[t][:].indirect(n3_t[:]), new[t][:])
            nc.sync.dma_start(out_rows[t], page[t][:])
            for c0, c1 in ((0, HALF), (HALF, U)) if t < 2 else ((0, HALF), (HALF, SPLIT), (SPLIT, U)):
                h = c0 // HALF
                src = page[t][:, c0:c1]
                dst = yb[h][:, c0 - HALF * h : c1 - HALF * h, :]
                if t == 2 and c0 < SPLIT:
                    nc.scalar.copy(dst[:, :, 2:4], src.unsqueeze(2).to_broadcast([P, c1 - c0, 2]))
                elif t == 3 and c0 < SPLIT:
                    nc.vector.tensor_copy(dst[:, :, t], src)
                else:
                    nc.scalar.copy(dst[:, :, t], src)

        y_words = sb([P, U], U32, "y_words")
        y_sc = sb([P, U], U8, "y_sc")
        for c0, c1 in ((0, HALF), (HALF, 768), (768, U)):
            cols = slice(c0, c1)
            h = c0 // HALF
            nc.vector.quantize_mx(
                out=y_words[:, cols].bitcast(FP8X4),
                scales=y_sc[:, cols],
                in_=yb[h][:, c0 - HALF * h : c1 - HALF * h, :].rearrange("p j t -> p (j t)"),
            )
            nc.sync.dma_start(words_of(out_1)[:, cols], y_words[:, cols].bitcast(I32))
        for q in range(4):
            eng = nc.scalar if q % 2 == 0 else nc.sync
            eng.dma_start(out_2[0, 4 * q : 4 * q + 4, :].bitcast(I32), y_sc[:].bitcast(I32)[32 * q : 32 * q + 4, :])
